import numpy as np
import ml_dtypes


def mxq(x, axis, fmt="e4m3"):
    dtype, down = {"e4m3": (ml_dtypes.float8_e4m3fn, 7), "e5m2": (ml_dtypes.float8_e5m2, 14)}[fmt]
    v = np.moveaxis(np.asarray(x, np.float32).astype(ml_dtypes.bfloat16).astype(np.float64), axis, -1)
    blocks = v.reshape(v.shape[:-1] + (-1, 32))
    amax = np.abs(blocks).max(-1, keepdims=True)
    byte = np.maximum(np.where(amax > 0, np.frexp(amax)[1] - 1 + 127, 0) - down, 1)
    scale = np.exp2(byte - 127.0)
    codes = (blocks / scale).astype(np.float32).astype(dtype).astype(np.float64)
    return np.moveaxis((codes * scale).reshape(v.shape), -1, axis)


WIDE = False


def mx_kscale(k):
    if not WIDE:
        return np.ones(k)
    levels = np.array([10, -10, 5, -5, 0])
    if k % 512:
        return np.exp2(np.random.permutation(np.resize(levels, k // 32))).repeat(32)
    a = np.empty((k // 512, 16))
    for p in range(k // 512):
        a[p, :8] = np.random.permutation(np.resize(levels, 8))
        for g in range(8):
            far = levels[np.abs(levels - a[p, g]) >= 10]
            a[p, g + 8] = far[np.random.randint(len(far))]
    return np.exp2(a.ravel()).repeat(32)


def f64(x):
    return np.asarray(x).astype(np.float64)


def striped(idx):
    return np.tile(np.asarray(idx).reshape(-1, 16).T, (8, 1)).astype(np.uint16)


def unstriped(offs):
    return offs[:16].T.reshape(-1).astype(np.int64)


def striped8(idx):
    return np.asarray(idx).reshape(8, -1, 16).transpose(0, 2, 1).reshape(128, -1).astype(np.uint16)


def unstriped8(offs):
    return offs.reshape(8, 16, -1).transpose(0, 2, 1).reshape(8, -1).astype(np.int64)


def pick8(x, idx, run):
    r = np.arange(len(x))
    return x[r[:, None], idx[r % (8 * run) // run]]


E2M1 = np.array([0.0, 0.5, 1.0, 1.5, 2.0, 3.0, 4.0, 6.0, -0.0, -0.5, -1.0, -1.5, -2.0, -3.0, -4.0, -6.0])


def pack_weight(w, fmt):
    k, n = w.shape
    w = f64(np.asarray(w, np.float32).astype(ml_dtypes.bfloat16)).reshape(k // 32, 32, n)
    amax = np.abs(w).max(1)
    if fmt == "e4m3":
        byte = np.frexp(amax)[1] - 1 + 127 - 7
    else:
        mant, ex = np.frexp(amax / 6.0)
        byte = np.where(mant > 0.5, ex, ex - 1) + 127
    byte = np.clip(np.where(amax > 0, byte, 1), 1, 254)
    scaled = (w * np.exp2(127.0 - byte)[:, None, :]).reshape(k, n).astype(np.float32)
    by_word = np.ascontiguousarray(scaled.reshape(k // 512, 128, 4, n).transpose(0, 1, 3, 2))
    if fmt == "e4m3":
        words = by_word.astype(ml_dtypes.float8_e4m3fn).view(np.uint8)
    else:
        c = by_word.astype(ml_dtypes.float4_e2m1fn).view(np.uint8) & 0xF
        words = (c[..., 0::2] | (c[..., 1::2] << 4)).reshape(k // 512, 128, 2 * n)
    return np.ascontiguousarray(words), np.ascontiguousarray(byte.astype(np.uint8).reshape(k // 512, 16, n))


def unpack_weight(words, scales, fmt):
    g, _, n = scales.shape
    words = np.ascontiguousarray(words).reshape(g, 128, n, -1)
    if fmt == "e4m3":
        vals = words.view(ml_dtypes.float8_e4m3fn).astype(np.float64)
    else:
        nib = np.empty((g, 128, n, 4), np.uint8)
        nib[..., 0::2] = words & 0xF
        nib[..., 1::2] = words >> 4
        vals = E2M1[nib]
    vals = vals * np.repeat(np.exp2(scales.astype(np.float64) - 127.0), 8, axis=1)[..., None]
    return vals.transpose(0, 1, 3, 2).reshape(g * 512, n)


K, J, R, T, F, G, O, N, U, E = 512, 512, 512, 2048, 2048, 1024, 256, 256, 128, 512


def setup_inputs():
    n = np.random.standard_normal
    idx = np.random.permutation(T)[:J]
    idx2 = np.stack([np.random.permutation(F)[:G] for _ in range(8)])
    idx3 = np.random.permutation(G)[:R]
    idx4 = np.stack([np.random.permutation(J)[:O] for _ in range(8)])
    idx5 = np.random.permutation(E)[:O]
    idx6 = np.stack([np.random.permutation(E)[:U] for _ in range(8)])
    idx7 = np.stack([np.random.permutation(O)[:U] for _ in range(8)])
    fk = mx_kscale(K)
    fr = mx_kscale(R)
    xtp = pack_weight(n((K, T)) * fk[:, None], "e2m1")
    wbp = pack_weight(n((R, N)) * 1 / np.sqrt(R) / fr[:, None], "e2m1")
    wop = pack_weight(n((R, N)) * 1 / np.sqrt(R) / fr[:, None], "e4m3")
    return {
        "xt_words": xtp[0],
        "xt_scales": xtp[1],
        "ua": (np.random.randint(-7, 8, (K, F)).astype(np.float64)).astype(np.float32),
        "ha": ((np.random.randint(8, 25, (K, 1)) / 1024.0) / fk[:, None]).astype(np.float32),
        "hb": (np.random.uniform(0.5, 1.6, (K, 1))).astype(np.float32),
        "sa": (np.random.uniform(0.5, 1.6, (R, 1)) * fr[:, None]).astype(np.float32),
        "wb_words": wbp[0],
        "wb_scales": wbp[1],
        "wo_words": wop[0],
        "wo_scales": wop[1],
        "so": (np.random.uniform(0.5, 1.6, (N, 1))).astype(np.float32),
        "sp": (np.random.uniform(0.5, 1.6, (N, 1))).astype(np.float32),
        "offs": striped(idx),
        "offs2": striped8(idx2),
        "offs3": striped(idx3),
        "offs4": striped8(idx4),
        "offs5": striped(idx5),
        "offs6": striped8(idx6),
        "offs7": striped8(idx7),
    }


def reference(xt_words, xt_scales, ua, ha, hb, sa, wb_words, wb_scales, wo_words, wo_scales, so, sp, offs, offs2, offs3, offs4, offs5, offs6, offs7):
    idx = unstriped(offs)
    idx2 = unstriped8(offs2)
    idx3 = unstriped(offs3)
    idx4 = unstriped8(offs4)
    idx5 = unstriped(offs5)
    idx6 = unstriped8(offs6)
    idx7 = unstriped8(offs7)
    xtu = unpack_weight(xt_words, xt_scales, "e2m1")
    wbu = unpack_weight(wb_words, wb_scales, "e2m1")
    wou = unpack_weight(wo_words, wo_scales, "e4m3")
    wcd = pick8(f64(ua), idx2, 64) * f64(ha)
    wc = wcd[:, idx3] * f64(hb)
    wcq = mxq(wc, 0, "e4m3")
    xtidxg = xtu[:, idx]
    a = wcq.T @ xtidxg
    g1 = np.maximum(a, 0.0)
    hid = pick8(g1, idx4, 64) * f64(sa)
    hidq = mxq(hid, 0, "e4m3")
    p = wbu.T @ hidq
    q = wou.T @ hidq
    m0 = np.zeros((N, E))
    m0[:, idx5] = p
    y = np.maximum(pick8(m0, idx6, 16) * f64(so), pick8(q, idx7, 16) * f64(sp))
    return y

@@ -1,0 +1,244 @@
+from contextlib import ExitStack
+
+import concourse.mybir as mybir
+
+K, J, R, T, F, G, O, N, U, E = 512, 512, 512, 2048, 2048, 1024, 256, 256, 128, 512
+FLOPS = 2 * K * R * J + 2 * 2 * R * N * O
+
+F32 = mybir.dt.float32
+BF16 = mybir.dt.bfloat16
+I32 = mybir.dt.int32
+U16 = mybir.dt.uint16
+U8 = mybir.dt.uint8
+FP8X4 = mybir.dt.float8_e4m3fn_x4
+FP4X4 = mybir.dt.float4_e2m1fn_x4
+ACT = mybir.ActivationFunctionType
+ALU = mybir.AluOpType
+
+P = 128
+PACK = 4
+LANES = 16
+
+
+def tile_picked_tokens_respelled_one_kept_outcomes_outboard_kernel(
+    tc, xt_words, xt_scales, ua, ha, hb, sa, wb_words, wb_scales, wo_words, wo_scales, so, sp,
+    offs, offs2, offs3, offs4, offs5, offs6, offs7, out,
+):
+    nc = tc.nc
+    with ExitStack() as ctx:
+        keep = ctx.enter_context(tc.tile_pool(name="keep", bufs=1))
+        psum = ctx.enter_context(tc.psum_pool(name="psum", bufs=1))
+
+        def sb(name, shape, dtype, tag=""):
+            return keep.tile(shape, dtype, name=name, tag=tag or name, align_bytes=64)
+
+        def load_list(name, src):
+            tile = keep.tile(list(src.shape), U16, name=name)
+            nc.sync.dma_start(tile[:], src)
+            return tile
+
+        def load_dealt(name, src):
+            tile = sb(name, [P, PACK], F32)
+            nc.sync.dma_start(tile[:], src.rearrange("(p t) o -> p (t o)", t=PACK))
+            return tile
+
+        def load_tiled(name, src):
+            tile = sb(name, [P, N // P], F32)
+            with nc.allow_non_contiguous_dma(reason="one value a partition for each block of 128 rows"):
+                nc.sync.dma_start(tile[:], src.rearrange("(i p) o -> p (i o)", p=P))
+            return tile
+
+        def load_scale_rows(name, src, width):
+            rows = sb(name + "_rows", [4, 4, width // 4], I32)
+            nc.sync.dma_start(rows[:], src[0].bitcast(I32).rearrange("(q r) c -> r q c", r=4))
+            return rows
+
+        def spread_scale_rows(name, rows, width):
+            plane = sb(name, [P, width], U8)
+            nc.vector.memset(plane[:].bitcast(I32), 0)
+            for q in range(4):
+                nc.vector.tensor_copy(plane[:].bitcast(I32)[32 * q : 32 * q + 4, :], rows[:, q, :])
+            return plane
+
+        ua_dealt = ua.rearrange("(p t) f -> t p f", t=PACK)
+        ua_rows = [sb("ua%d" % t, [P, F], F32) for t in range(PACK)]
+        list2 = load_list("list2", offs2)
+        nc.sync.dma_start(ua_rows[0][:], ua_dealt[0])
+        ha_sb = load_dealt("ha_sb", ha)
+        nc.sync.dma_start(ua_rows[1][:], ua_dealt[1])
+        list3 = load_list("list3", offs3)
+        hb_sb = load_dealt("hb_sb", hb)
+        nc.sync.dma_start(ua_rows[2][:], ua_dealt[2])
+        xw = sb("xw", [P, T], U16)
+        nc.sync.dma_start(xw[:].bitcast(I32), xt_words[0].bitcast(I32))
+        list1 = load_list("list1", offs)
+        xs_rows = load_scale_rows("xs", xt_scales, T)
+        wbs_rows = load_scale_rows("wbs", wb_scales, N)
+        wos_rows = load_scale_rows("wos", wo_scales, N)
+        nc.sync.dma_start(ua_rows[3][:], ua_dealt[3])
+        list4 = load_list("list4", offs4)
+        sa_sb = load_dealt("sa_sb", sa)
+        wbw = sb("wbw", [P, 2 * N], U8)
+        nc.sync.dma_start(wbw[:].bitcast(I32), wb_words[0].bitcast(I32))
+        wow = sb("wow", [P, N], I32)
+        nc.sync.dma_start(wow[:], wo_words[0].rearrange("p n t -> p (n t)").bitcast(I32))
+        list5 = load_list("list5", offs5)
+        list6 = load_list("list6", offs6)
+        list7 = load_list("list7", offs7)
+        so_sb = load_tiled("so_sb", so)
+        sp_sb = load_tiled("sp_sb", sp)
+
+        boards = [sb("board%d" % i, [P, E], F32) for i in range(N // P)]
+        for board in boards:
+            nc.vector.memset(board[:], 0.0)
+
+        xs = spread_scale_rows("xs", xs_rows, T)
+        xg_words = sb("xg_words", [P, J], U16)
+        xg_scales = sb("xg_scales", [P, J], U8)
+        nc.vector.tensor_copy(xg_words[:], xw[:].indirect(list1[:]))
+        nc.vector.tensor_copy(xg_scales[:], xs[:].indirect(list1[:]))
+        wbs = spread_scale_rows("wbs", wbs_rows, N)
+        wos = spread_scale_rows("wos", wos_rows, N)
+
+        HR = R // 2
+        HM = HR // PACK
+        wc_in = [sb("wc_in%d" % h, [P, PACK, HM, PACK], BF16) for h in range(2)]
+        wc_words = [sb("wc_words%d" % j, [P, P], I32) for j in range(PACK)]
+        wc_scales = [sb("wc_scales%d" % j, [P, P], U8) for j in range(PACK)]
+
+        def quantise_wc(h, j):
+            cols = slice(h * HM, (h + 1) * HM)
+            nc.vector.quantize_mx(
+                out=wc_words[j][:, cols].bitcast(FP8X4),
+                scales=wc_scales[j][:, cols],
+                in_=wc_in[h][:, j].rearrange("p m t -> p (m t)"),
+            )
+
+        wcd = [sb("wcd%d" % t, [P, G], F32) for t in range(PACK)]
+        pairs = {}
+
+        def spell(t):
+            nc.scalar.activation(wcd[t][:], ua_rows[t][:].indirect(list2[:]), ACT.Copy, scale=ha_sb[:, t : t + 1])
+
+        def read_words(t, h):
+            part = list3[:, h * HR // LANES : (h + 1) * HR // LANES]
+            nc.scalar.activation(pairs[t // 2, h][:, t % 2, :], wcd[t][:].indirect(part), ACT.Copy, scale=hb_sb[:, t : t + 1])
+
+        def weave(u, h, j):
+            return wc_in[h][:, j, :, 2 * u : 2 * u + 2], pairs[u, h][:].rearrange("p e (m j) -> p j m e", j=PACK)[:, j]
+
+        every = slice(0, PACK)
+        spell(0)
+        spell(1)
+        pairs[0, 0] = sb("wc00", [P, 2, HR], BF16)
+        read_words(0, 0)
+        read_words(1, 0)
+        nc.vector.tensor_copy(*weave(0, 0, every))
+        spell(2)
+        pairs[0, 1] = sb("wc01", [P, 2, HR], BF16, "ua2")
+        read_words(0, 1)
+        read_words(1, 1)
+        nc.vector.tensor_copy(*weave(0, 1, every))
+        spell(3)
+        upper = sb("wc1", [P, 2, 2, HR], BF16, "ua3")
+        pairs[1, 0], pairs[1, 1] = upper[:, 0], upper[:, 1]
+        read_words(2, 0)
+        read_words(3, 0)
+        nc.vector.tensor_copy(*weave(1, 0, every))
+        for j in range(PACK):
+            quantise_wc(0, j)
+        read_words(2, 1)
+        read_words(3, 1)
+        nc.vector.tensor_copy(*weave(1, 1, 0))
+        nc.vector.tensor_copy(*weave(1, 1, 1))
+        nc.scalar.copy(*weave(1, 1, 2))
+        nc.scalar.copy(*weave(1, 1, 3))
+        for j in range(PACK):
+            quantise_wc(1, j)
+
+        HJ = J // 2
+        HO = O // 2
+        hid01 = sb("hid01", [P, 2, O], BF16)
+        hid_words = sb("hid_words", [P, O], I32)
+        hid_scales = sb("hid_scales", [P, O], U8)
+        g1 = [sb("g1_%d" % j, [P, J], F32) for j in range(PACK)]
+        halves4 = [list4[:, h * HO // LANES : (h + 1) * HO // LANES] for h in range(2)]
+
+        def take(dst, j, offsets):
+            nc.scalar.activation(dst, g1[j][:].indirect(offsets), ACT.Copy, scale=sa_sb[:, j : j + 1])
+
+        for j in range(PACK):
+            for h in range(2):
+                cols = slice(h * HJ, (h + 1) * HJ)
+                acc = psum.tile([P, HJ], F32, name="acc%d_%d" % (j, h), tag="bank%d" % (2 * j + h))
+                nc.tensor.matmul_mx(
+                    out=acc[:], lhsT=wc_words[j][:].bitcast(FP8X4), lhsT_scale=wc_scales[j][:],
+                    rhs=xg_words[:, cols].bitcast(FP4X4), rhs_scale=xg_scales[:, cols], start=True, stop=True,
+                )
+                if j == 0 and h == 1:
+                    nc.scalar.activation(g1[j][:, cols], acc[:], ACT.Relu)
+                else:
+                    nc.vector.tensor_scalar_max(g1[j][:, cols], acc[:], 0.0)
+            if j < 2:
+                take(hid01[:, j, :], j, list4[:])
+
+        hid_in = sb("hid_in", [P, O, PACK], BF16, "wc_words3")
+        nc.vector.tensor_copy(hid_in[:, :, 0:2], hid01[:].rearrange("p e o -> p o e"))
+        for h in range(2):
+            cols = slice(h * HO, (h + 1) * HO)
+            hid23 = sb("hid23_%d" % h, [P, 2, HO], BF16, "hid01" if h == 1 else "")
+            for j in (2, 3):
+                take(hid23[:, j - 2, :], j, halves4[h])
+            nc.vector.tensor_copy(hid_in[:, cols, 2:4], hid23[:].rearrange("p e o -> p o e"))
+            nc.vector.quantize_mx(
+                out=hid_words[:, cols].bitcast(FP8X4), scales=hid_scales[:, cols],
+                in_=hid_in[:, cols, :].rearrange("p o t -> p (o t)"),
+            )
+
+        NT = N // P
+        p_acc = [psum.tile([P, NT, HO], F32, name="p_acc%d" % h, tag="bank%d" % h) for h in range(2)]
+        q_acc = [psum.tile([P, O], F32, name="q_acc%d" % i, tag="bank%d" % (2 + i)) for i in range(NT)]
+        for h in range(2):
+            cols = slice(h * HO, (h + 1) * HO)
+            for i in range(NT):
+                nc.tensor.matmul_mx(
+                    out=p_acc[h][:, i, :], lhsT=wbw[:, 2 * P * i : 2 * P * (i + 1)].bitcast(FP4X4),
+                    lhsT_scale=wbs[:, P * i : P * (i + 1)],
+                    rhs=hid_words[:, cols].bitcast(FP8X4), rhs_scale=hid_scales[:, cols], start=True, stop=True,
+                )
+        for i in (1, 0):
+            nc.tensor.matmul_mx(
+                out=q_acc[i][:], lhsT=wow[:, P * i : P * (i + 1)].bitcast(FP8X4), lhsT_scale=wos[:, P * i : P * (i + 1)],
+                rhs=hid_words[:].bitcast(FP8X4), rhs_scale=hid_scales[:], start=True, stop=True,
+            )
+
+        p_sb = [sb("p_sb%d" % h, [P, NT, HO], F32) for h in range(2)]
+        q_sb = [sb("q_sb%d" % i, [P, O], F32) for i in range(NT)]
+        first = [sb("first%d" % i, [P, U], F32) for i in range(NT)]
+        second = [sb("second%d" % i, [P, U], F32) for i in range(NT)]
+        halves5 = [list5[:, h * HO // LANES : (h + 1) * HO // LANES] for h in range(2)]
+
+        def fetch_first(i):
+            nc.scalar.activation(first[i][:], boards[i][:].indirect(list6[:]), ACT.Copy, scale=so_sb[:, i : i + 1])
+
+        def fetch_second(i):
+            nc.scalar.activation(second[i][:], q_sb[i][:].indirect(list7[:]), ACT.Copy, scale=sp_sb[:, i : i + 1])
+
+        def finish(i):
+            larger = sb("larger%d" % i, [P, U], F32)
+            nc.vector.tensor_tensor(larger[:], first[i][:], second[i][:], ALU.max)
+            nc.sync.dma_start(out[P * i : P * (i + 1), :], larger[:])
+
+        nc.scalar.copy(p_sb[0][:], p_acc[0][:])
+        nc.vector.tensor_copy(p_sb[1][:], p_acc[1][:])
+        nc.vector.tensor_copy(q_sb[1][:], q_acc[1][:])
+        for h in range(2):
+            nc.scalar.activation(boards[1][:].indirect(halves5[h]), p_sb[h][:, 1, :], ACT.Copy)
+            nc.vector.tensor_copy(boards[0][:].indirect(halves5[h]), p_sb[h][:, 0, :])
+        nc.vector.tensor_copy(q_sb[0][:], q_acc[0][:])
+        fetch_second(1)
+        fetch_first(1)
+        fetch_first(0)
+        fetch_second(0)
+        finish(1)
+        finish(0)

@@ -88,6 +88,10 @@ def tile_picked_tokens_respelled_one_kept_outcomes_outboard_kernel(
         so_sb = load_tiled("so_sb", so)
         sp_sb = load_tiled("sp_sb", sp)
 
+        idle = sb("idle", [P, 2], F32)
+        nc.vector.memset(idle[:, 0:1], 0.0)
+        nc.scalar.activation(idle[:, 1:2], idle[:, 0:1], ACT.Copy)
+
         boards = [sb("board%d" % i, [P, E], F32) for i in range(N // P)]
         for board in boards:
             nc.vector.memset(board[:], 0.0)

@@ -62,8 +62,8 @@ def tile_picked_tokens_respelled_one_kept_outcomes_outboard_kernel(
 
         ua_dealt = ua.rearrange("(p t) f -> t p f", t=PACK)
         ua_rows = [sb("ua%d" % t, [P, F], F32) for t in range(PACK)]
-        list2 = load_list("list2", offs2)
         nc.sync.dma_start(ua_rows[0][:], ua_dealt[0])
+        list2 = load_list("list2", offs2)
         ha_sb = load_dealt("ha_sb", ha)
         nc.sync.dma_start(ua_rows[1][:], ua_dealt[1])
         list3 = load_list("list3", offs3)
@@ -92,6 +92,8 @@ def tile_picked_tokens_respelled_one_kept_outcomes_outboard_kernel(
         nc.vector.memset(idle[:, 0:1], 0.0)
         nc.scalar.activation(idle[:, 1:2], idle[:, 0:1], ACT.Copy)
 
+        floor = sb("floor", [P, 1], F32)
+        nc.vector.memset(floor[:], 0.0)
         boards = [sb("board%d" % i, [P, E], F32) for i in range(N // P)]
         for board in boards:
             nc.vector.memset(board[:], 0.0)
@@ -153,12 +155,11 @@ def tile_picked_tokens_respelled_one_kept_outcomes_outboard_kernel(
             quantise_wc(0, j)
         read_words(2, 1)
         read_words(3, 1)
-        nc.vector.tensor_copy(*weave(1, 1, 0))
-        nc.vector.tensor_copy(*weave(1, 1, 1))
-        nc.scalar.copy(*weave(1, 1, 2))
-        nc.scalar.copy(*weave(1, 1, 3))
-        for j in range(PACK):
-            quantise_wc(1, j)
+        for j in range(PACK + 1):
+            if j < PACK:
+                nc.vector.tensor_copy(*weave(1, 1, j))
+            if j > 0:
+                quantise_wc(1, j - 1)
 
         HJ = J // 2
         HO = O // 2
@@ -171,22 +172,26 @@ def tile_picked_tokens_respelled_one_kept_outcomes_outboard_kernel(
         def take(dst, j, offsets):
             nc.scalar.activation(dst, g1[j][:].indirect(offsets), ACT.Copy, scale=sa_sb[:, j : j + 1])
 
+        bank = 0
         for j in range(PACK):
-            for h in range(2):
-                cols = slice(h * HJ, (h + 1) * HJ)
-                acc = psum.tile([P, HJ], F32, name="acc%d_%d" % (j, h), tag="bank%d" % (2 * j + h))
+            pieces = 4 if j == 0 else 2
+            width = J // pieces
+            for h in range(pieces):
+                cols = slice(h * width, (h + 1) * width)
+                acc = psum.tile([P, width], F32, name="acc%d_%d" % (j, h), tag="bank%d" % (bank % 8))
+                bank = bank + 1
                 nc.tensor.matmul_mx(
                     out=acc[:], lhsT=wc_words[j][:].bitcast(FP8X4), lhsT_scale=wc_scales[j][:],
                     rhs=xg_words[:, cols].bitcast(FP4X4), rhs_scale=xg_scales[:, cols], start=True, stop=True,
                 )
-                if j == 0 and h == 1:
+                if j == 0 and h % 2 == 0:
                     nc.scalar.activation(g1[j][:, cols], acc[:], ACT.Relu)
                 else:
-                    nc.vector.tensor_scalar_max(g1[j][:, cols], acc[:], 0.0)
+                    nc.vector.tensor_scalar_max(g1[j][:, cols], acc[:], floor[:])
             if j < 2:
                 take(hid01[:, j, :], j, list4[:])
 
-        hid_in = sb("hid_in", [P, O, PACK], BF16, "wc_words3")
+        hid_in = sb("hid_in", [P, O, PACK], BF16, "floor")
         nc.vector.tensor_copy(hid_in[:, :, 0:2], hid01[:].rearrange("p e o -> p o e"))
         for h in range(2):
             cols = slice(h * HO, (h + 1) * HO)
@@ -200,24 +205,33 @@ def tile_picked_tokens_respelled_one_kept_outcomes_outboard_kernel(
             )
 
         NT = N // P
-        p_acc = [psum.tile([P, NT, HO], F32, name="p_acc%d" % h, tag="bank%d" % h) for h in range(2)]
-        q_acc = [psum.tile([P, O], F32, name="q_acc%d" % i, tag="bank%d" % (2 + i)) for i in range(NT)]
-        for h in range(2):
+        p_sb = {(h, i): sb("p_sb%d_%d" % (h, i), [P, HO], F32) for h in range(2) for i in range(NT)}
+        q_sb = [sb("q_sb%d" % i, [P, O], F32) for i in range(NT)]
+        p_acc, q_acc = {}, {}
+
+        def multiply(h):
             cols = slice(h * HO, (h + 1) * HO)
             for i in range(NT):
+                p_acc[h, i] = psum.tile([P, HO], F32, name="p_acc%d_%d" % (h, i), tag="bank%d" % (2 + i))
                 nc.tensor.matmul_mx(
-                    out=p_acc[h][:, i, :], lhsT=wbw[:, 2 * P * i : 2 * P * (i + 1)].bitcast(FP4X4),
+                    out=p_acc[h, i][:], lhsT=wbw[:, 2 * P * i : 2 * P * (i + 1)].bitcast(FP4X4),
                     lhsT_scale=wbs[:, P * i : P * (i + 1)],
                     rhs=hid_words[:, cols].bitcast(FP8X4), rhs_scale=hid_scales[:, cols], start=True, stop=True,
                 )
-        for i in (1, 0):
-            nc.tensor.matmul_mx(
-                out=q_acc[i][:], lhsT=wow[:, P * i : P * (i + 1)].bitcast(FP8X4), lhsT_scale=wos[:, P * i : P * (i + 1)],
-                rhs=hid_words[:].bitcast(FP8X4), rhs_scale=hid_scales[:], start=True, stop=True,
-            )
+            for i in range(NT):
+                q_acc[h, i] = psum.tile([P, HO], F32, name="q_acc%d_%d" % (h, i), tag="bank%d" % (4 + i))
+                nc.tensor.matmul_mx(
+                    out=q_acc[h, i][:], lhsT=wow[:, P * i : P * (i + 1)].bitcast(FP8X4), lhsT_scale=wos[:, P * i : P * (i + 1)],
+                    rhs=hid_words[:, cols].bitcast(FP8X4), rhs_scale=hid_scales[:, cols], start=True, stop=True,
+                )
 
-        p_sb = [sb("p_sb%d" % h, [P, NT, HO], F32) for h in range(2)]
-        q_sb = [sb("q_sb%d" % i, [P, O], F32) for i in range(NT)]
+        multiply(0)
+        for i in range(NT):
+            nc.scalar.copy(p_sb[0, i][:], p_acc[0, i][:])
+        for i in range(NT):
+            nc.scalar.copy(q_sb[i][:, 0:HO], q_acc[0, i][:])
+        multiply(1)
+
         first = [sb("first%d" % i, [P, U], F32) for i in range(NT)]
         second = [sb("second%d" % i, [P, U], F32) for i in range(NT)]
         halves5 = [list5[:, h * HO // LANES : (h + 1) * HO // LANES] for h in range(2)]
@@ -233,16 +247,16 @@ def tile_picked_tokens_respelled_one_kept_outcomes_outboard_kernel(
             nc.vector.tensor_tensor(larger[:], first[i][:], second[i][:], ALU.max)
             nc.sync.dma_start(out[P * i : P * (i + 1), :], larger[:])
 
-        nc.scalar.copy(p_sb[0][:], p_acc[0][:])
-        nc.vector.tensor_copy(p_sb[1][:], p_acc[1][:])
-        nc.vector.tensor_copy(q_sb[1][:], q_acc[1][:])
-        for h in range(2):
-            nc.scalar.activation(boards[1][:].indirect(halves5[h]), p_sb[h][:, 1, :], ACT.Copy)
-            nc.vector.tensor_copy(boards[0][:].indirect(halves5[h]), p_sb[h][:, 0, :])
-        nc.vector.tensor_copy(q_sb[0][:], q_acc[0][:])
-        fetch_second(1)
-        fetch_first(1)
-        fetch_first(0)
-        fetch_second(0)
-        finish(1)
-        finish(0)
+        nc.vector.tensor_copy(boards[0][:].indirect(halves5[0]), p_sb[0, 0][:])
+        nc.scalar.activation(boards[1][:].indirect(halves5[0]), p_sb[0, 1][:], ACT.Copy)
+        for i in range(NT):
+            nc.vector.tensor_copy(p_sb[1, i][:], p_acc[1, i][:])
+        nc.scalar.activation(boards[0][:].indirect(halves5[1]), p_sb[1, 0][:], ACT.Copy)
+        for i in range(NT):
+            nc.vector.tensor_copy(q_sb[i][:, HO:O], q_acc[1, i][:])
+        nc.vector.tensor_copy(boards[1][:].indirect(halves5[1]), p_sb[1, 1][:])
+        for i in range(NT):
+            fetch_second(i)
+        for i in range(NT):
+            fetch_first(i)
+            finish(i)

from contextlib import ExitStack

import concourse.mybir as mybir

K, J, R, T, F, G, O, N, U, E = 512, 512, 512, 2048, 2048, 1024, 256, 256, 128, 512
FLOPS = 2 * K * R * J + 2 * 2 * R * N * O

F32 = mybir.dt.float32
BF16 = mybir.dt.bfloat16
I32 = mybir.dt.int32
U16 = mybir.dt.uint16
U8 = mybir.dt.uint8
FP8X4 = mybir.dt.float8_e4m3fn_x4
FP4X4 = mybir.dt.float4_e2m1fn_x4
ACT = mybir.ActivationFunctionType
ALU = mybir.AluOpType

P = 128
PACK = 4
LANES = 16


def tile_picked_tokens_respelled_one_kept_outcomes_outboard_kernel(
    tc, xt_words, xt_scales, ua, ha, hb, sa, wb_words, wb_scales, wo_words, wo_scales, so, sp,
    offs, offs2, offs3, offs4, offs5, offs6, offs7, out,
):
    nc = tc.nc
    with ExitStack() as ctx:
        keep = ctx.enter_context(tc.tile_pool(name="keep", bufs=1))
        psum = ctx.enter_context(tc.psum_pool(name="psum", bufs=1))

        def sb(name, shape, dtype, tag=""):
            return keep.tile(shape, dtype, name=name, tag=tag or name, align_bytes=64)

        def load_list(name, src):
            tile = keep.tile(list(src.shape), U16, name=name)
            nc.sync.dma_start(tile[:], src)
            return tile

        def load_dealt(name, src):
            tile = sb(name, [P, PACK], F32)
            nc.sync.dma_start(tile[:], src.rearrange("(p t) o -> p (t o)", t=PACK))
            return tile

        def load_tiled(name, src):
            tile = sb(name, [P, N // P], F32)
            with nc.allow_non_contiguous_dma(reason="one value a partition for each block of 128 rows"):
                nc.sync.dma_start(tile[:], src.rearrange("(i p) o -> p (i o)", p=P))
            return tile

        def load_scale_rows(name, src, width):
            rows = sb(name + "_rows", [4, 4, width // 4], I32)
            nc.sync.dma_start(rows[:], src[0].bitcast(I32).rearrange("(q r) c -> r q c", r=4))
            return rows

        def spread_scale_rows(name, rows, width):
            plane = sb(name, [P, width], U8)
            nc.vector.memset(plane[:].bitcast(I32), 0)
            for q in range(4):
                nc.vector.tensor_copy(plane[:].bitcast(I32)[32 * q : 32 * q + 4, :], rows[:, q, :])
            return plane

        ua_dealt = ua.rearrange("(p t) f -> t p f", t=PACK)
        ua_rows = [sb("ua%d" % t, [P, F], F32) for t in range(PACK)]
        nc.sync.dma_start(ua_rows[0][:], ua_dealt[0])
        list2 = load_list("list2", offs2)
        ha_sb = load_dealt("ha_sb", ha)
        nc.sync.dma_start(ua_rows[1][:], ua_dealt[1])
        list3 = load_list("list3", offs3)
        hb_sb = load_dealt("hb_sb", hb)
        nc.sync.dma_start(ua_rows[2][:], ua_dealt[2])
        xw = sb("xw", [P, T], U16)
        nc.sync.dma_start(xw[:].bitcast(I32), xt_words[0].bitcast(I32))
        list1 = load_list("list1", offs)
        xs_rows = load_scale_rows("xs", xt_scales, T)
        wbs_rows = load_scale_rows("wbs", wb_scales, N)
        wos_rows = load_scale_rows("wos", wo_scales, N)
        nc.sync.dma_start(ua_rows[3][:], ua_dealt[3])
        list4 = load_list("list4", offs4)
        sa_sb = load_dealt("sa_sb", sa)
        wbw = sb("wbw", [P, 2 * N], U8)
        nc.sync.dma_start(wbw[:].bitcast(I32), wb_words[0].bitcast(I32))
        wow = sb("wow", [P, N], I32)
        nc.sync.dma_start(wow[:], wo_words[0].rearrange("p n t -> p (n t)").bitcast(I32))
        list5 = load_list("list5", offs5)
        list6 = load_list("list6", offs6)
        list7 = load_list("list7", offs7)
        so_sb = load_tiled("so_sb", so)
        sp_sb = load_tiled("sp_sb", sp)

        idle = sb("idle", [P, 2], F32)
        nc.vector.memset(idle[:, 0:1], 0.0)
        nc.scalar.activation(idle[:, 1:2], idle[:, 0:1], ACT.Copy)

        floor = sb("floor", [P, 1], F32)
        nc.vector.memset(floor[:], 0.0)
        boards = [sb("board%d" % i, [P, E], F32) for i in range(N // P)]
        for board in boards:
            nc.vector.memset(board[:], 0.0)

        xs = spread_scale_rows("xs", xs_rows, T)
        xg_words = sb("xg_words", [P, J], U16)
        xg_scales = sb("xg_scales", [P, J], U8)
        nc.vector.tensor_copy(xg_words[:], xw[:].indirect(list1[:]))
        nc.vector.tensor_copy(xg_scales[:], xs[:].indirect(list1[:]))
        wbs = spread_scale_rows("wbs", wbs_rows, N)
        wos = spread_scale_rows("wos", wos_rows, N)

        HR = R // 2
        HM = HR // PACK
        wc_in = [sb("wc_in%d" % h, [P, PACK, HM, PACK], BF16) for h in range(2)]
        wc_words = [sb("wc_words%d" % j, [P, P], I32) for j in range(PACK)]
        wc_scales = [sb("wc_scales%d" % j, [P, P], U8) for j in range(PACK)]

        def quantise_wc(h, j):
            cols = slice(h * HM, (h + 1) * HM)
            nc.vector.quantize_mx(
                out=wc_words[j][:, cols].bitcast(FP8X4),
                scales=wc_scales[j][:, cols],
                in_=wc_in[h][:, j].rearrange("p m t -> p (m t)"),
            )

        wcd = [sb("wcd%d" % t, [P, G], F32) for t in range(PACK)]
        pairs = {}

        def spell(t):
            nc.scalar.activation(wcd[t][:], ua_rows[t][:].indirect(list2[:]), ACT.Copy, scale=ha_sb[:, t : t + 1])

        def read_words(t, h):
            part = list3[:, h * HR // LANES : (h + 1) * HR // LANES]
            nc.scalar.activation(pairs[t // 2, h][:, t % 2, :], wcd[t][:].indirect(part), ACT.Copy, scale=hb_sb[:, t : t + 1])

        def weave(u, h, j):
            return wc_in[h][:, j, :, 2 * u : 2 * u + 2], pairs[u, h][:].rearrange("p e (m j) -> p j m e", j=PACK)[:, j]

        every = slice(0, PACK)
        spell(0)
        spell(1)
        pairs[0, 0] = sb("wc00", [P, 2, HR], BF16)
        read_words(0, 0)
        read_words(1, 0)
        nc.vector.tensor_copy(*weave(0, 0, every))
        spell(2)
        pairs[0, 1] = sb("wc01", [P, 2, HR], BF16, "ua2")
        read_words(0, 1)
        read_words(1, 1)
        nc.vector.tensor_copy(*weave(0, 1, every))
        spell(3)
        upper = sb("wc1", [P, 2, 2, HR], BF16, "ua3")
        pairs[1, 0], pairs[1, 1] = upper[:, 0], upper[:, 1]
        read_words(2, 0)
        read_words(3, 0)
        nc.vector.tensor_copy(*weave(1, 0, every))
        for j in range(PACK):
            quantise_wc(0, j)
        read_words(2, 1)
        read_words(3, 1)
        for j in range(PACK + 1):
            if j < PACK:
                nc.vector.tensor_copy(*weave(1, 1, j))
            if j > 0:
                quantise_wc(1, j - 1)

        HJ = J // 2
        HO = O // 2
        hid01 = sb("hid01", [P, 2, O], BF16)
        hid_words = sb("hid_words", [P, O], I32)
        hid_scales = sb("hid_scales", [P, O], U8)
        g1 = [sb("g1_%d" % j, [P, J], F32) for j in range(PACK)]
        halves4 = [list4[:, h * HO // LANES : (h + 1) * HO // LANES] for h in range(2)]

        def take(dst, j, offsets):
            nc.scalar.activation(dst, g1[j][:].indirect(offsets), ACT.Copy, scale=sa_sb[:, j : j + 1])

        bank = 0
        for j in range(PACK):
            pieces = 4 if j == 0 else 2
            width = J // pieces
            for h in range(pieces):
                cols = slice(h * width, (h + 1) * width)
                acc = psum.tile([P, width], F32, name="acc%d_%d" % (j, h), tag="bank%d" % (bank % 8))
                bank = bank + 1
                nc.tensor.matmul_mx(
                    out=acc[:], lhsT=wc_words[j][:].bitcast(FP8X4), lhsT_scale=wc_scales[j][:],
                    rhs=xg_words[:, cols].bitcast(FP4X4), rhs_scale=xg_scales[:, cols], start=True, stop=True,
                )
                if j == 0 and h % 2 == 0:
                    nc.scalar.activation(g1[j][:, cols], acc[:], ACT.Relu)
                else:
                    nc.vector.tensor_scalar_max(g1[j][:, cols], acc[:], floor[:])
            if j < 2:
                take(hid01[:, j, :], j, list4[:])

        hid_in = sb("hid_in", [P, O, PACK], BF16, "floor")
        nc.vector.tensor_copy(hid_in[:, :, 0:2], hid01[:].rearrange("p e o -> p o e"))
        for h in range(2):
            cols = slice(h * HO, (h + 1) * HO)
            hid23 = sb("hid23_%d" % h, [P, 2, HO], BF16, "hid01" if h == 1 else "")
            for j in (2, 3):
                take(hid23[:, j - 2, :], j, halves4[h])
            nc.vector.tensor_copy(hid_in[:, cols, 2:4], hid23[:].rearrange("p e o -> p o e"))
            nc.vector.quantize_mx(
                out=hid_words[:, cols].bitcast(FP8X4), scales=hid_scales[:, cols],
                in_=hid_in[:, cols, :].rearrange("p o t -> p (o t)"),
            )

        NT = N // P
        p_sb = {(h, i): sb("p_sb%d_%d" % (h, i), [P, HO], F32) for h in range(2) for i in range(NT)}
        q_sb = [sb("q_sb%d" % i, [P, O], F32) for i in range(NT)]
        p_acc, q_acc = {}, {}

        def multiply(h):
            cols = slice(h * HO, (h + 1) * HO)
            for i in range(NT):
                p_acc[h, i] = psum.tile([P, HO], F32, name="p_acc%d_%d" % (h, i), tag="bank%d" % (2 + i))
                nc.tensor.matmul_mx(
                    out=p_acc[h, i][:], lhsT=wbw[:, 2 * P * i : 2 * P * (i + 1)].bitcast(FP4X4),
                    lhsT_scale=wbs[:, P * i : P * (i + 1)],
                    rhs=hid_words[:, cols].bitcast(FP8X4), rhs_scale=hid_scales[:, cols], start=True, stop=True,
                )
            for i in range(NT):
                q_acc[h, i] = psum.tile([P, HO], F32, name="q_acc%d_%d" % (h, i), tag="bank%d" % (4 + i))
                nc.tensor.matmul_mx(
                    out=q_acc[h, i][:], lhsT=wow[:, P * i : P * (i + 1)].bitcast(FP8X4), lhsT_scale=wos[:, P * i : P * (i + 1)],
                    rhs=hid_words[:, cols].bitcast(FP8X4), rhs_scale=hid_scales[:, cols], start=True, stop=True,
                )

        multiply(0)
        for i in range(NT):
            nc.scalar.copy(p_sb[0, i][:], p_acc[0, i][:])
        for i in range(NT):
            nc.scalar.copy(q_sb[i][:, 0:HO], q_acc[0, i][:])
        multiply(1)

        first = [sb("first%d" % i, [P, U], F32) for i in range(NT)]
        second = [sb("second%d" % i, [P, U], F32) for i in range(NT)]
        halves5 = [list5[:, h * HO // LANES : (h + 1) * HO // LANES] for h in range(2)]

        def fetch_first(i):
            nc.scalar.activation(first[i][:], boards[i][:].indirect(list6[:]), ACT.Copy, scale=so_sb[:, i : i + 1])

        def fetch_second(i):
            nc.scalar.activation(second[i][:], q_sb[i][:].indirect(list7[:]), ACT.Copy, scale=sp_sb[:, i : i + 1])

        def finish(i):
            larger = sb("larger%d" % i, [P, U], F32)
            nc.vector.tensor_tensor(larger[:], first[i][:], second[i][:], ALU.max)
            nc.sync.dma_start(out[P * i : P * (i + 1), :], larger[:])

        nc.vector.tensor_copy(boards[0][:].indirect(halves5[0]), p_sb[0, 0][:])
        nc.scalar.activation(boards[1][:].indirect(halves5[0]), p_sb[0, 1][:], ACT.Copy)
        for i in range(NT):
            nc.vector.tensor_copy(p_sb[1, i][:], p_acc[1, i][:])
        nc.scalar.activation(boards[0][:].indirect(halves5[1]), p_sb[1, 0][:], ACT.Copy)
        for i in range(NT):
            nc.vector.tensor_copy(q_sb[i][:, HO:O], q_acc[1, i][:])
        nc.vector.tensor_copy(boards[1][:].indirect(halves5[1]), p_sb[1, 1][:])
        for i in range(NT):
            fetch_second(i)
        for i in range(NT):
            fetch_first(i)
            finish(i)
